import numpy as np
import ml_dtypes


def mxq(x, axis, fmt="e4m3"):
    dtype, down = {"e4m3": (ml_dtypes.float8_e4m3fn, 7), "e5m2": (ml_dtypes.float8_e5m2, 14)}[fmt]
    v = np.moveaxis(np.asarray(x, np.float32).astype(ml_dtypes.bfloat16).astype(np.float64), axis, -1)
    blocks = v.reshape(v.shape[:-1] + (-1, 32))
    amax = np.abs(blocks).max(-1, keepdims=True)
    byte = np.maximum(np.where(amax > 0, np.frexp(amax)[1] - 1 + 127, 0) - down, 1)
    scale = np.exp2(byte - 127.0)
    codes = (blocks / scale).astype(np.float32).astype(dtype).astype(np.float64)
    return np.moveaxis((codes * scale).reshape(v.shape), -1, axis)


WIDE = False


def mx_kscale(k):
    if not WIDE:
        return np.ones(k)
    levels = np.array([10, -10, 5, -5, 0])
    if k % 512:
        return np.exp2(np.random.permutation(np.resize(levels, k // 32))).repeat(32)
    a = np.empty((k // 512, 16))
    for p in range(k // 512):
        a[p, :8] = np.random.permutation(np.resize(levels, 8))
        for g in range(8):
            far = levels[np.abs(levels - a[p, g]) >= 10]
            a[p, g + 8] = far[np.random.randint(len(far))]
    return np.exp2(a.ravel()).repeat(32)


def f64(x):
    return np.asarray(x).astype(np.float64)


def striped(idx):
    return np.tile(idx.reshape(-1, 16).T, (8, 1)).astype(np.uint16)


def unstriped(offs):
    return offs[:16].T.reshape(-1).astype(np.int64)


E2M1 = np.array([0.0, 0.5, 1.0, 1.5, 2.0, 3.0, 4.0, 6.0, -0.0, -0.5, -1.0, -1.5, -2.0, -3.0, -4.0, -6.0])


def pack_weight(w, fmt):
    k, n = w.shape
    w = f64(np.asarray(w, np.float32).astype(ml_dtypes.bfloat16)).reshape(k // 32, 32, n)
    amax = np.abs(w).max(1)
    if fmt == "e4m3":
        byte = np.frexp(amax)[1] - 1 + 127 - 7
    else:
        mant, ex = np.frexp(amax / 6.0)
        byte = np.where(mant > 0.5, ex, ex - 1) + 127
    byte = np.clip(np.where(amax > 0, byte, 1), 1, 254)
    scaled = (w * np.exp2(127.0 - byte)[:, None, :]).reshape(k, n).astype(np.float32)
    by_word = np.ascontiguousarray(scaled.reshape(k // 512, 128, 4, n).transpose(0, 1, 3, 2))
    if fmt == "e4m3":
        words = by_word.astype(ml_dtypes.float8_e4m3fn).view(np.uint8)
    else:
        c = by_word.astype(ml_dtypes.float4_e2m1fn).view(np.uint8) & 0xF
        words = (c[..., 0::2] | (c[..., 1::2] << 4)).reshape(k // 512, 128, 2 * n)
    return np.ascontiguousarray(words), np.ascontiguousarray(byte.astype(np.uint8).reshape(k // 512, 16, n))


def unpack_weight(words, scales, fmt):
    g, _, n = scales.shape
    words = np.ascontiguousarray(words).reshape(g, 128, n, -1)
    if fmt == "e4m3":
        vals = words.view(ml_dtypes.float8_e4m3fn).astype(np.float64)
    else:
        nib = np.empty((g, 128, n, 4), np.uint8)
        nib[..., 0::2] = words & 0xF
        nib[..., 1::2] = words >> 4
        vals = E2M1[nib]
    vals = vals * np.repeat(np.exp2(scales.astype(np.float64) - 127.0), 8, axis=1)[..., None]
    return vals.transpose(0, 1, 3, 2).reshape(g * 512, n)


def gelu(v):
    return 0.5 * v * (1.0 + np.tanh(np.sqrt(2.0 / np.pi) * (v + 0.044715 * v**3)))


K, H, T, S, T2, P = 1024, 1024, 2048, 512, 1024, 512

def setup_inputs():
    n = np.random.standard_normal
    s, u = mx_kscale(K)[:, None], mx_kscale(H)[:, None]
    tab_words, tab_scales = pack_weight(n((K, T)) * s, "e4m3")
    w1_words, w1_scales = pack_weight(n((K, H)) / np.sqrt(K) / s * u.T, "e2m1")
    w3_words, w3_scales = pack_weight(n((K, H)) / np.sqrt(K) / s * u.T, "e4m3")
    return {
        "tab_words": tab_words, "tab_scales": tab_scales,
        "offs": striped(np.random.permutation(T)[:S]),
        "w1_words": w1_words, "w1_scales": w1_scales,
        "w2": (n((K, H)) / np.sqrt(K) / s * u.T).astype(np.float32),
        "w3_words": w3_words, "w3_scales": w3_scales,
        "page0": (n((H, T2)) * u).astype(np.float32),
        "wgs": np.exp(0.3 * n((128, S))).astype(np.float32),
        "offs2": striped(np.random.permutation(T2)[:S]),
        "offs3": striped(np.random.permutation(T2)[:P]),
        "offs4": striped(np.random.permutation(T2)[:P]),
        "bd": (n(H) * u[:, 0]).astype(np.float32),
        "gd": (np.sign(n(H)) * np.exp(0.3 * n(H)) / np.sqrt(H) / u[:, 0] ** 2).astype(np.float32),
        "rv": n(P).astype(np.float32),
        "mat": np.exp(0.5 * n((P, P))).astype(np.float32),
    }

def reference(tab_words, tab_scales, offs, w1_words, w1_scales, w2, w3_words, w3_scales, page0, wgs, offs2, offs3, offs4, bd, gd, rv, mat):
    v = unpack_weight(tab_words, tab_scales, "e4m3")[:, unstriped(offs)]
    y1 = unpack_weight(w1_words, w1_scales, "e2m1").T @ v
    y2 = mxq(f64(w2), 0, "e4m3").T @ v
    y3 = unpack_weight(w3_words, w3_scales, "e4m3").T @ v
    h = np.maximum(y1, y2) + np.minimum(y1, y3)
    page = f64(page0).copy()
    page[:, unstriped(offs2)] = np.tile(f64(wgs), (H // 128, 1)) * h
    x1 = page[:, unstriped(offs3)]
    x2 = (page[:, unstriped(offs4)] + f64(bd)[:, None]) * f64(gd)[:, None]
    e = mxq(x1, 0, "e4m3").T @ mxq(x2, 0, "e4m3")
    return (e + f64(rv)[:, None]) * f64(mat)

@@ -1,0 +1,310 @@
+from contextlib import ExitStack
+
+import concourse.mybir as mybir
+from concourse.masks import make_identity
+
+K, H, T, S, T2, NP = 1024, 1024, 2048, 512, 1024, 512
+FLOPS = 3 * 2 * K * H * S + 2 * H * NP * NP
+
+F32 = mybir.dt.float32
+BF16 = mybir.dt.bfloat16
+I32 = mybir.dt.int32
+U32 = mybir.dt.uint32
+U16 = mybir.dt.uint16
+U8 = mybir.dt.uint8
+FP8X4 = mybir.dt.float8_e4m3fn_x4
+FP4X4 = mybir.dt.float4_e2m1fn_x4
+ALU = mybir.AluOpType
+ACT = mybir.ActivationFunctionType
+
+P = 128
+PACK = 4
+PASS = P * PACK
+KP = K // PASS
+HP = H // PASS
+JT = S // P
+MT = NP // P
+QUAD = 4
+
+
+def interleave(copy, dst, src):
+    copy(
+        out=dst.rearrange("p (c i) t -> p c t i", i=4),
+        in_=src.rearrange("p t (c i) -> p c t i", i=4),
+    )
+
+
+def tile_list_freezedry_deviation_match_kernel(
+    tc, tab_words, tab_scales, offs, w1_words, w1_scales, w2, w3_words, w3_scales,
+    page0, wgs, offs2, offs3, offs4, bd, gd, rv, mat, out,
+):
+    nc = tc.nc
+    with ExitStack() as ctx:
+        keep = ctx.enter_context(tc.tile_pool(name="keep", bufs=1))
+        psum = ctx.enter_context(tc.psum_pool(name="psum", bufs=1))
+
+        def tile(shape, dtype, name, tag=None):
+            return keep.tile(shape, dtype, name=name, tag=tag or name, align_bytes=64)
+
+        lists = {}
+        for name in ("offs", "offs2", "offs3", "offs4"):
+            lists[name] = tile([P, S // 16], U16, "list_" + name)
+        bank = [psum.tile([P, PASS], F32, name="bank%d" % i) for i in range(8)]
+
+        tab_w = [tile([P, T], U32, "tab_w%d" % a) for a in range(KP)]
+        tab_s = tile([P, KP, T], U8, "tab_s")
+        v_w = [tile([P, S], U32, "v_w%d" % a) for a in range(KP)]
+        v_s = [tile([P, S], U8, "v_s%d" % a) for a in range(KP)]
+        w1_w = [tile([P, KP, 2 * PASS], U8, "w1_w%d" % b) for b in range(HP)]
+        w3_w = [tile([P, KP, PASS], U32, "w3_w%d" % b) for b in range(HP)]
+        w1_s = tile([P, KP, H], U8, "w1_s")
+        w3_s = tile([P, KP, H], U8, "w3_s")
+        w2_raw = {(b, a): tile([P, PACK, PASS], F32, "w2_raw%d%d" % (b, a)) for b in range(HP) for a in range(KP)}
+        w2_bf = [tile([P, PASS, PACK], BF16, "w2_bf%d" % a) for a in range(KP)]
+        w2_w = {(b, a): tile([P, PASS], U32, "w2_w%d%d" % (b, a)) for b in range(HP) for a in range(KP)}
+        w2_s = {(b, a): tile([P, PASS], U8, "w2_s%d%d" % (b, a)) for b in range(HP) for a in range(KP)}
+        y1 = [tile([P, PACK, P], F32, "y1_%d" % j) for j in range(JT)]
+        low = [tile([P, PACK, P], F32, "low%d" % j) for j in range(JT)]
+        high = {(0, j): tile([P, S], F32, "high%d" % j) for j in range(JT)}
+        h = {(0, t): tile([P, S], F32, "h%d" % t) for t in range(PACK)}
+        for i in range(PACK):
+            high[1, i], h[1, i] = high[0, i], h[0, i]
+        high[1, 0], h[1, 2] = h[0, 2], high[0, 0]
+        page = {(b, t): tile([P, T2], F32, "page%d%d" % (b, t)) for b in range(HP) for t in range(PACK)}
+        wg = [tile([P, S], F32, "wg0"), tile([P, PACK - 1, S], F32, "wg_rest")]
+        picked = {(b, t): tile([P, NP], F32, "picked%d%d" % (b, t)) for b in range(HP) for t in range(PACK)}
+        shifted = [tile([P, NP], F32, "shifted%d" % i) for i in range(2)]
+        x1_planes = [tile([P, PACK, NP], BF16, "x1_planes0")]
+        x1_bf = [tile([P, NP, PACK], BF16, "x1_bf%d" % b) for b in range(HP)]
+        x2_bf = [tile([P, NP, PACK], BF16, "x2_bf%d" % b) for b in range(HP)]
+        x1_w = [tile([P, NP], U32, "x1_w%d" % b) for b in range(HP)]
+        x2_w = [tile([P, NP], U32, "x2_w%d" % b) for b in range(HP)]
+        x1_s = [tile([P, NP], U8, "x1_s%d" % b) for b in range(HP)]
+        x2_s = [tile([P, NP], U8, "x2_s%d" % b) for b in range(HP)]
+        bd_t = tile([P, HP, PACK], F32, "bd_t")
+        gd_t = tile([P, HP, PACK], F32, "gd_t")
+        rv_t = tile([P, MT], F32, "rv_t")
+        ident = tile([P, P], F32, "ident")
+
+        def wgs_plane(t):
+            return wg[0][:] if t == 0 else wg[1][:, t - 1, :]
+
+        def load_scales(queue, dst, src):
+            for q in range(QUAD):
+                queue.dma_start(
+                    out=dst[32 * q : 32 * q + 4, :, :].bitcast(I32),
+                    in_=src[:, 4 * q : 4 * q + 4, :].rearrange("a r c -> r a c").bitcast(I32),
+                )
+
+        def load_table(a):
+            nc.sync.dma_start(out=tab_w[a][:].bitcast(I32), in_=tab_words[a].rearrange("p t i -> p (t i)").bitcast(I32))
+
+        def load_packed_weights(b):
+            nc.sync.dma_start(
+                out=w1_w[b][:].bitcast(I32),
+                in_=w1_words[:, :, 2 * PASS * b : 2 * PASS * (b + 1)].rearrange("a p c -> p a c").bitcast(I32),
+            )
+            nc.sync.dma_start(
+                out=w3_w[b][:].bitcast(I32),
+                in_=w3_words[:, :, PASS * b : PASS * (b + 1), :].rearrange("a p c i -> p a (c i)").bitcast(I32),
+            )
+
+        def load_w2(b, a):
+            nc.sync.dma_start(
+                out=w2_raw[b, a][:],
+                in_=w2[PASS * a : PASS * (a + 1), PASS * b : PASS * (b + 1)].rearrange("(p i) c -> p i c", i=PACK),
+            )
+
+        def load_page(b, t):
+            rows = page0[PASS * b : PASS * (b + 1), :].rearrange("(p t) c -> p t c", t=PACK)
+            nc.sync.dma_start(out=page[b, t][:], in_=rows[:, t, :])
+
+        wgs_rows = wgs.rearrange("(q t) c -> q t c", t=PACK)
+
+        nc.vector.memset(tab_s[:].bitcast(I32), 0)
+        nc.vector.memset(w1_s[:].bitcast(I32), 0)
+        nc.vector.memset(w3_s[:].bitcast(I32), 0)
+        nc.sync.dma_start(lists["offs"][:], offs)
+        load_table(0)
+        load_scales(nc.sync, tab_s, tab_scales)
+        load_packed_weights(0)
+        load_scales(nc.sync, w1_s, w1_scales)
+        load_table(1)
+        load_w2(0, 0)
+        load_scales(nc.sync, w3_s, w3_scales)
+        load_w2(0, 1)
+        load_page(0, 0)
+        nc.sync.dma_start(lists["offs2"][:], offs2)
+        for q in range(QUAD):
+            nc.sync.dma_start(out=wg[0][32 * q : 32 * (q + 1), :], in_=wgs_rows[:, 0, :])
+        nc.sync.dma_start(lists["offs4"][:], offs4)
+        nc.sync.dma_start(lists["offs3"][:], offs3)
+        for q in range(QUAD):
+            nc.sync.dma_start(out=wg[1][32 * q : 32 * (q + 1), :, :], in_=wgs_rows[:, 1:PACK, :])
+        load_page(0, 1)
+        load_packed_weights(1)
+        load_w2(1, 0)
+        load_w2(1, 1)
+        nc.sync.dma_start(out=bd_t[:], in_=bd.rearrange("(b p t) -> p b t", b=HP, t=PACK))
+        nc.sync.dma_start(out=gd_t[:], in_=gd.rearrange("(b p t) -> p b t", b=HP, t=PACK))
+        for b, t in ((1, 0), (1, 1), (0, 2), (0, 3), (1, 2), (1, 3)):
+            load_page(b, t)
+        make_identity(nc, ident[:])
+
+        for a in range(KP):
+            nc.vector.tensor_copy(v_w[a][:], tab_w[a][:].indirect(lists["offs"][:]))
+            nc.vector.tensor_copy(v_s[a][:], tab_s[:, a, :].indirect(lists["offs"][:]))
+
+        def first_stage(dst, j, rhs, rhs_scale):
+            cols = slice(P * j, P * (j + 1))
+            for a in range(KP):
+                nc.tensor.matmul_mx(
+                    out=dst[:], lhsT=v_w[a][:, cols].bitcast(FP8X4), lhsT_scale=v_s[a][:, cols],
+                    rhs=rhs(a), rhs_scale=rhs_scale(a), start=(a == 0), stop=(a == KP - 1),
+                )
+
+        def dealt(b_):
+            return b_[:].rearrange("p (q t) -> p t q", t=PACK)
+
+        def planes(flat):
+            return flat[:].rearrange("p (t q) -> p t q", t=PACK)
+
+        def minima(b):
+            cols = slice(PASS * b, PASS * (b + 1))
+            for j in range(JT):
+                first_stage(bank[j], j, lambda a: w1_w[b][:, a, :].bitcast(FP4X4), lambda a: w1_s[:, a, cols])
+                first_stage(bank[4 + j], j, lambda a: w3_w[b][:, a, :].bitcast(FP8X4), lambda a: w3_s[:, a, cols])
+                nc.scalar.copy(out=y1[j][:], in_=dealt(bank[j]))
+                nc.vector.tensor_tensor(low[j][:], dealt(bank[4 + j]), y1[j][:], ALU.min)
+
+        def quantise_w2(b, a, copy):
+            interleave(copy, w2_bf[a][:], w2_raw[b, a][:])
+            nc.vector.quantize_mx(
+                out=w2_w[b, a][:].bitcast(FP8X4), scales=w2_s[b, a][:],
+                in_=w2_bf[a][:].rearrange("p c i -> p (c i)"),
+            )
+
+        def maxima(b):
+            for j in range(JT):
+                first_stage(bank[j], j, lambda a: w2_w[b, a][:].bitcast(FP8X4), lambda a: w2_s[b, a][:])
+                nc.vector.tensor_tensor(planes(high[b, j]), dealt(bank[j]), y1[j][:], ALU.max)
+
+        def features(b, t, j0=0, j1=JT):
+            terms = [(term, j) for j in range(j0, j1) for term in (planes(high[b, j]), low[j][:])]
+            for n, (term, j) in enumerate(terms):
+                nc.tensor.matmul(
+                    out=bank[4 + t][:, P * j : P * (j + 1)], lhsT=term[:, t, :], rhs=ident[:],
+                    is_transpose=True, start=(n == 0), stop=(n == len(terms) - 1),
+                )
+            nc.scalar.copy(out=h[b, t][:, P * j0 : P * j1], in_=bank[4 + t][:, P * j0 : P * j1])
+
+        def put(b, t, j0=0, j1=JT):
+            cols = slice(P * j0, P * j1)
+            entries = lists["offs2"][:, P * j0 // 16 : P * j1 // 16]
+            nc.vector.tensor_tensor(page[b, t][:].indirect(entries), h[b, t][:, cols], wgs_plane(t)[:, cols], ALU.mult)
+
+        def pick_classes(b, t):
+            nc.vector.tensor_copy(picked[b, t][:], page[b, t][:].indirect(lists["offs4"][:]))
+
+        def put_and_pick_classes(b, t):
+            put(b, t)
+            pick_classes(b, t)
+
+        def finish_classes(b, t):
+            tmp = high[1, JT - 1] if (b, t) == (0, PACK - 1) else shifted[t % 2]
+            nc.scalar.activation(out=tmp[:], in_=picked[b, t][:], func=ACT.Identity, bias=bd_t[:, b, t : t + 1], scale=1.0)
+            nc.scalar.activation(out=x2_bf[b][:, :, t], in_=tmp[:], func=ACT.Copy, scale=gd_t[:, b, t : t + 1])
+
+        def pick_runs(b, t, m0, m1):
+            nc.vector.tensor_copy(x1_planes[b][:, t, m0:m1], page[b, t][:].indirect(lists["offs3"][:, m0 // 16 : m1 // 16]))
+
+        def quantise_runs(b, m0, m1):
+            interleave(nc.scalar.copy, x1_bf[b][:, m0:m1, :], x1_planes[b][:, :, m0:m1])
+            nc.vector.quantize_mx(
+                out=x1_w[b][:, m0:m1].bitcast(FP8X4), scales=x1_s[b][:, m0:m1],
+                in_=x1_bf[b][:, m0:m1, :].rearrange("p c i -> p (c i)"),
+            )
+
+        def quantise_classes(b):
+            nc.vector.quantize_mx(
+                out=x2_w[b][:].bitcast(FP8X4), scales=x2_s[b][:], in_=x2_bf[b][:].rearrange("p c i -> p (c i)"),
+            )
+
+        def match(b, m):
+            cols = slice(P * m, P * (m + 1))
+            nc.tensor.matmul_mx(
+                out=bank[m][:], lhsT=x1_w[b][:, cols].bitcast(FP8X4), lhsT_scale=x1_s[b][:, cols],
+                rhs=x2_w[b][:].bitcast(FP8X4), rhs_scale=x2_s[b][:], start=(b == 0), stop=(b == HP - 1),
+            )
+
+        quantise_w2(0, 0, nc.vector.tensor_copy)
+        minima(0)
+        quantise_w2(0, 1, nc.scalar.copy)
+        maxima(0)
+        features(0, 0, 0, JT // 2)
+        features(0, 0, JT // 2, JT)
+        for t in range(1, PACK):
+            features(0, t)
+        put(0, 0, 0, JT // 2)
+        put(0, 0, JT // 2, JT)
+        pick_classes(0, 0)
+        pick_runs(0, 0, 0, NP)
+        put_and_pick_classes(0, 1)
+        pick_runs(0, 1, 0, NP)
+        minima(1)
+        for a in range(KP):
+            quantise_w2(1, a, nc.scalar.copy)
+        put_and_pick_classes(0, 2)
+        pick_runs(0, 2, 0, NP)
+        for t in (0, 1, 2):
+            finish_classes(0, t)
+        maxima(1)
+        put_and_pick_classes(0, 3)
+        pick_runs(0, 3, 0, NP)
+        for t in range(PACK):
+            features(1, t)
+        finish_classes(0, 3)
+
+        x1_planes.append(tile([P, PACK, NP], BF16, "x1_planes1", tag="wg_rest"))
+        mat_t = tile([P, MT, NP], F32, "mat_t", tag="w2_raw00")
+        result = tile([P, MT, NP], F32, "result", tag="w2_raw01")
+        with nc.allow_non_contiguous_dma(reason="one value a partition"):
+            nc.sync.dma_start(out=rv_t[:], in_=rv.rearrange("(m p) -> p m", p=P))
+        nc.sync.dma_start(out=mat_t[:], in_=mat.rearrange("(m p) j -> p m j", p=P))
+
+        put_and_pick_classes(1, 0)
+        quantise_runs(0, 0, NP)
+        finish_classes(1, 0)
+        quantise_classes(0)
+        for m in range(MT):
+            match(0, m)
+        for t in range(1, PACK):
+            put_and_pick_classes(1, t)
+            finish_classes(1, t)
+        chunks = [(0, 2), (2, 3), (3, 4)]
+
+        def pick_chunk(m0, m1):
+            for t in range(PACK):
+                pick_runs(1, t, P * m0, P * m1)
+
+        def finish(m):
+            nc.vector.scalar_tensor_tensor(
+                out=result[:, m, :], in0=bank[m][:], scalar=rv_t[:, m : m + 1], in1=mat_t[:, m, :],
+                op0=ALU.add, op1=ALU.mult,
+            )
+            nc.sync.dma_start(out=out[P * m : P * (m + 1), :], in_=result[:, m, :])
+
+        def match_chunk(m0, m1):
+            quantise_runs(1, P * m0, P * m1)
+            for m in range(m0, m1):
+                match(1, m)
+
+        pick_chunk(*chunks[0])
+        quantise_classes(1)
+        pick_chunk(*chunks[1])
+        match_chunk(*chunks[0])
+        pick_chunk(*chunks[2])
+        match_chunk(*chunks[1])
+        match_chunk(*chunks[2])
+        for m in range(MT):
+            finish(m)

@@ -25,6 +25,7 @@ HP = H // PASS
 JT = S // P
 MT = NP // P
 QUAD = 4
+CHUNKS = ((0, 2), (2, 3), (3, 4))
 
 
 def interleave(copy, dst, src):
@@ -57,25 +58,32 @@ def tile_list_freezedry_deviation_match_kernel(
         v_s = [tile([P, S], U8, "v_s%d" % a) for a in range(KP)]
         w1_w = [tile([P, KP, 2 * PASS], U8, "w1_w%d" % b) for b in range(HP)]
         w3_w = [tile([P, KP, PASS], U32, "w3_w%d" % b) for b in range(HP)]
-        w1_s = tile([P, KP, H], U8, "w1_s")
-        w3_s = tile([P, KP, H], U8, "w3_s")
-        w2_raw = {(b, a): tile([P, PACK, PASS], F32, "w2_raw%d%d" % (b, a)) for b in range(HP) for a in range(KP)}
+        w1_s = [tile([P, KP, PASS], U8, "w1_s%d" % b) for b in range(HP)]
+        w3_s = [tile([P, KP, PASS], U8, "w3_s%d" % b) for b in range(HP)]
+        w2_raw = {}
+        for b in range(HP):
+            for a in range(KP):
+                width = PASS // 2 if (b, a) == (0, KP - 1) else PASS
+                w2_raw[b, a] = [
+                    (slice(c, c + width), tile([P, PACK, width], F32, "w2_raw%d%d_%d" % (b, a, c)))
+                    for c in range(0, PASS, width)
+                ]
         w2_bf = [tile([P, PASS, PACK], BF16, "w2_bf%d" % a) for a in range(KP)]
         w2_w = {(b, a): tile([P, PASS], U32, "w2_w%d%d" % (b, a)) for b in range(HP) for a in range(KP)}
         w2_s = {(b, a): tile([P, PASS], U8, "w2_s%d%d" % (b, a)) for b in range(HP) for a in range(KP)}
-        y1 = [tile([P, PACK, P], F32, "y1_%d" % j) for j in range(JT)]
-        low = [tile([P, PACK, P], F32, "low%d" % j) for j in range(JT)]
+        y1 = [tile([P, 2, P, 2], F32, "y1_%d" % j) for j in range(JT)]
+        low = [tile([P, 2, P, 2], F32, "low%d" % j)[:] for j in range(JT)]
         high = {(0, j): tile([P, S], F32, "high%d" % j) for j in range(JT)}
         h = {(0, t): tile([P, S], F32, "h%d" % t) for t in range(PACK)}
         for i in range(PACK):
             high[1, i], h[1, i] = high[0, i], h[0, i]
         high[1, 0], h[1, 2] = h[0, 2], high[0, 0]
         page = {(b, t): tile([P, T2], F32, "page%d%d" % (b, t)) for b in range(HP) for t in range(PACK)}
-        wg = [tile([P, S], F32, "wg0"), tile([P, PACK - 1, S], F32, "wg_rest")]
+        wg = [tile([P, S], F32, "wg0"), tile([P, S], F32, "wg1"), tile([P, 2, S], F32, "wg_rest")]
         picked = {(b, t): tile([P, NP], F32, "picked%d%d" % (b, t)) for b in range(HP) for t in range(PACK)}
-        shifted = [tile([P, NP], F32, "shifted%d" % i) for i in range(2)]
-        x1_planes = [tile([P, PACK, NP], BF16, "x1_planes0")]
-        x1_bf = [tile([P, NP, PACK], BF16, "x1_bf%d" % b) for b in range(HP)]
+        shifted = tile([P, NP], F32, "shifted")
+        x1_planes = {(0, 0): tile([P, PACK, NP], BF16, "x1_planes0")}
+        x1_bf = {(0, 0): tile([P, NP, PACK], BF16, "x1_bf0")}
         x2_bf = [tile([P, NP, PACK], BF16, "x2_bf%d" % b) for b in range(HP)]
         x1_w = [tile([P, NP], U32, "x1_w%d" % b) for b in range(HP)]
         x2_w = [tile([P, NP], U32, "x2_w%d" % b) for b in range(HP)]
@@ -87,11 +95,11 @@ def tile_list_freezedry_deviation_match_kernel(
         ident = tile([P, P], F32, "ident")
 
         def wgs_plane(t):
-            return wg[0][:] if t == 0 else wg[1][:, t - 1, :]
+            return wg[t][:] if t < 2 else wg[2][:, t - 2, :]
 
-        def load_scales(queue, dst, src):
+        def load_scales(dst, src):
             for q in range(QUAD):
-                queue.dma_start(
+                nc.sync.dma_start(
                     out=dst[32 * q : 32 * q + 4, :, :].bitcast(I32),
                     in_=src[:, 4 * q : 4 * q + 4, :].rearrange("a r c -> r a c").bitcast(I32),
                 )
@@ -99,21 +107,22 @@ def tile_list_freezedry_deviation_match_kernel(
         def load_table(a):
             nc.sync.dma_start(out=tab_w[a][:].bitcast(I32), in_=tab_words[a].rearrange("p t i -> p (t i)").bitcast(I32))
 
-        def load_packed_weights(b):
+        def load_w1(b):
             nc.sync.dma_start(
                 out=w1_w[b][:].bitcast(I32),
                 in_=w1_words[:, :, 2 * PASS * b : 2 * PASS * (b + 1)].rearrange("a p c -> p a c").bitcast(I32),
             )
+
+        def load_w3(b):
             nc.sync.dma_start(
                 out=w3_w[b][:].bitcast(I32),
                 in_=w3_words[:, :, PASS * b : PASS * (b + 1), :].rearrange("a p c i -> p a (c i)").bitcast(I32),
             )
 
         def load_w2(b, a):
-            nc.sync.dma_start(
-                out=w2_raw[b, a][:],
-                in_=w2[PASS * a : PASS * (a + 1), PASS * b : PASS * (b + 1)].rearrange("(p i) c -> p i c", i=PACK),
-            )
+            rows = w2[PASS * a : PASS * (a + 1), PASS * b : PASS * (b + 1)].rearrange("(p i) c -> p i c", i=PACK)
+            for cols, raw in w2_raw[b, a]:
+                nc.sync.dma_start(out=raw[:], in_=rows[:, :, cols])
 
         def load_page(b, t):
             rows = page0[PASS * b : PASS * (b + 1), :].rearrange("(p t) c -> p t c", t=PACK)
@@ -122,32 +131,39 @@ def tile_list_freezedry_deviation_match_kernel(
         wgs_rows = wgs.rearrange("(q t) c -> q t c", t=PACK)
 
         nc.vector.memset(tab_s[:].bitcast(I32), 0)
-        nc.vector.memset(w1_s[:].bitcast(I32), 0)
-        nc.vector.memset(w3_s[:].bitcast(I32), 0)
+        for b in range(HP):
+            nc.vector.memset(w1_s[b][:].bitcast(I32), 0)
+            nc.vector.memset(w3_s[b][:].bitcast(I32), 0)
         nc.sync.dma_start(lists["offs"][:], offs)
         load_table(0)
-        load_scales(nc.sync, tab_s, tab_scales)
-        load_packed_weights(0)
-        load_scales(nc.sync, w1_s, w1_scales)
+        load_scales(tab_s, tab_scales)
+        load_w1(0)
         load_table(1)
+        load_scales(w1_s[0], w1_scales[:, :, :PASS])
         load_w2(0, 0)
-        load_scales(nc.sync, w3_s, w3_scales)
+        load_w3(0)
+        load_scales(w3_s[0], w3_scales[:, :, :PASS])
         load_w2(0, 1)
         load_page(0, 0)
         nc.sync.dma_start(lists["offs2"][:], offs2)
         for q in range(QUAD):
             nc.sync.dma_start(out=wg[0][32 * q : 32 * (q + 1), :], in_=wgs_rows[:, 0, :])
+        for q in range(QUAD):
+            nc.sync.dma_start(out=wg[1][32 * q : 32 * (q + 1), :], in_=wgs_rows[:, 1, :])
+        load_page(0, 1)
         nc.sync.dma_start(lists["offs4"][:], offs4)
         nc.sync.dma_start(lists["offs3"][:], offs3)
+        load_w1(1)
+        load_scales(w1_s[1], w1_scales[:, :, PASS:])
+        load_w3(1)
+        load_scales(w3_s[1], w3_scales[:, :, PASS:])
         for q in range(QUAD):
-            nc.sync.dma_start(out=wg[1][32 * q : 32 * (q + 1), :, :], in_=wgs_rows[:, 1:PACK, :])
-        load_page(0, 1)
-        load_packed_weights(1)
+            nc.sync.dma_start(out=wg[2][32 * q : 32 * (q + 1), :, :], in_=wgs_rows[:, 2:PACK, :])
         load_w2(1, 0)
         load_w2(1, 1)
         nc.sync.dma_start(out=bd_t[:], in_=bd.rearrange("(b p t) -> p b t", b=HP, t=PACK))
         nc.sync.dma_start(out=gd_t[:], in_=gd.rearrange("(b p t) -> p b t", b=HP, t=PACK))
-        for b, t in ((1, 0), (1, 1), (0, 2), (0, 3), (1, 2), (1, 3)):
+        for b, t in ((1, 0), (0, 2), (1, 1), (0, 3), (1, 2), (1, 3)):
             load_page(b, t)
         make_identity(nc, ident[:])
 
@@ -164,21 +180,21 @@ def tile_list_freezedry_deviation_match_kernel(
                 )
 
         def dealt(b_):
-            return b_[:].rearrange("p (q t) -> p t q", t=PACK)
+            return b_[:].rearrange("p (q s e) -> p s q e", s=2, e=2)
 
         def planes(flat):
-            return flat[:].rearrange("p (t q) -> p t q", t=PACK)
+            return flat[:].rearrange("p (s q e) -> p s q e", s=2, e=2)
 
         def minima(b):
-            cols = slice(PASS * b, PASS * (b + 1))
             for j in range(JT):
-                first_stage(bank[j], j, lambda a: w1_w[b][:, a, :].bitcast(FP4X4), lambda a: w1_s[:, a, cols])
-                first_stage(bank[4 + j], j, lambda a: w3_w[b][:, a, :].bitcast(FP8X4), lambda a: w3_s[:, a, cols])
+                first_stage(bank[j], j, lambda a: w1_w[b][:, a, :].bitcast(FP4X4), lambda a: w1_s[b][:, a, :])
+                first_stage(bank[4 + j], j, lambda a: w3_w[b][:, a, :].bitcast(FP8X4), lambda a: w3_s[b][:, a, :])
                 nc.scalar.copy(out=y1[j][:], in_=dealt(bank[j]))
-                nc.vector.tensor_tensor(low[j][:], dealt(bank[4 + j]), y1[j][:], ALU.min)
+                nc.vector.tensor_tensor(low[j], dealt(bank[4 + j]), y1[j][:], ALU.min)
 
         def quantise_w2(b, a, copy):
-            interleave(copy, w2_bf[a][:], w2_raw[b, a][:])
+            for cols, raw in w2_raw[b, a]:
+                interleave(copy, w2_bf[a][:, cols, :], raw[:])
             nc.vector.quantize_mx(
                 out=w2_w[b, a][:].bitcast(FP8X4), scales=w2_s[b, a][:],
                 in_=w2_bf[a][:].rearrange("p c i -> p (c i)"),
@@ -186,17 +202,20 @@ def tile_list_freezedry_deviation_match_kernel(
 
         def maxima(b):
             for j in range(JT):
-                first_stage(bank[j], j, lambda a: w2_w[b, a][:].bitcast(FP8X4), lambda a: w2_s[b, a][:])
-                nc.vector.tensor_tensor(planes(high[b, j]), dealt(bank[j]), y1[j][:], ALU.max)
+                first_stage(bank[4 + j], j, lambda a: w2_w[b, a][:].bitcast(FP8X4), lambda a: w2_s[b, a][:])
+                nc.vector.tensor_tensor(planes(high[b, j]), dealt(bank[4 + j]), y1[j][:], ALU.max)
 
-        def features(b, t, j0=0, j1=JT):
-            terms = [(term, j) for j in range(j0, j1) for term in (planes(high[b, j]), low[j][:])]
+        def features(b, t, acc, j0=0, j1=JT, minima_first=False):
+            if minima_first:
+                terms = [(low[j], j) for j in range(j0, j1)] + [(planes(high[b, j]), j) for j in range(j0, j1)]
+            else:
+                terms = [(term, j) for j in range(j0, j1) for term in (planes(high[b, j]), low[j])]
             for n, (term, j) in enumerate(terms):
                 nc.tensor.matmul(
-                    out=bank[4 + t][:, P * j : P * (j + 1)], lhsT=term[:, t, :], rhs=ident[:],
+                    out=acc[:, P * j : P * (j + 1)], lhsT=term[:, t // 2, :, t % 2], rhs=ident[:],
                     is_transpose=True, start=(n == 0), stop=(n == len(terms) - 1),
                 )
-            nc.scalar.copy(out=h[b, t][:, P * j0 : P * j1], in_=bank[4 + t][:, P * j0 : P * j1])
+            nc.scalar.copy(out=h[b, t][:, P * j0 : P * j1], in_=acc[:, P * j0 : P * j1])
 
         def put(b, t, j0=0, j1=JT):
             cols = slice(P * j0, P * j1)
@@ -211,18 +230,17 @@ def tile_list_freezedry_deviation_match_kernel(
             pick_classes(b, t)
 
         def finish_classes(b, t):
-            tmp = high[1, JT - 1] if (b, t) == (0, PACK - 1) else shifted[t % 2]
-            nc.scalar.activation(out=tmp[:], in_=picked[b, t][:], func=ACT.Identity, bias=bd_t[:, b, t : t + 1], scale=1.0)
-            nc.scalar.activation(out=x2_bf[b][:, :, t], in_=tmp[:], func=ACT.Copy, scale=gd_t[:, b, t : t + 1])
+            nc.scalar.activation(out=shifted[:], in_=picked[b, t][:], func=ACT.Identity, bias=bd_t[:, b, t : t + 1], scale=1.0)
+            nc.scalar.activation(out=x2_bf[b][:, :, t], in_=shifted[:], func=ACT.Copy, scale=gd_t[:, b, t : t + 1])
 
         def pick_runs(b, t, m0, m1):
-            nc.vector.tensor_copy(x1_planes[b][:, t, m0:m1], page[b, t][:].indirect(lists["offs3"][:, m0 // 16 : m1 // 16]))
+            nc.vector.tensor_copy(x1_planes[b, m0][:, t, :], page[b, t][:].indirect(lists["offs3"][:, m0 // 16 : m1 // 16]))
 
         def quantise_runs(b, m0, m1):
-            interleave(nc.scalar.copy, x1_bf[b][:, m0:m1, :], x1_planes[b][:, :, m0:m1])
+            interleave(nc.scalar.copy, x1_bf[b, m0][:], x1_planes[b, m0][:])
             nc.vector.quantize_mx(
                 out=x1_w[b][:, m0:m1].bitcast(FP8X4), scales=x1_s[b][:, m0:m1],
-                in_=x1_bf[b][:, m0:m1, :].rearrange("p c i -> p (c i)"),
+                in_=x1_bf[b, m0][:].rearrange("p c i -> p (c i)"),
             )
 
         def quantise_classes(b):
@@ -233,7 +251,7 @@ def tile_list_freezedry_deviation_match_kernel(
         def match(b, m):
             cols = slice(P * m, P * (m + 1))
             nc.tensor.matmul_mx(
-                out=bank[m][:], lhsT=x1_w[b][:, cols].bitcast(FP8X4), lhsT_scale=x1_s[b][:, cols],
+                out=bank[4 + m][:], lhsT=x1_w[b][:, cols].bitcast(FP8X4), lhsT_scale=x1_s[b][:, cols],
                 rhs=x2_w[b][:].bitcast(FP8X4), rhs_scale=x2_s[b][:], start=(b == 0), stop=(b == HP - 1),
             )
 
@@ -241,33 +259,35 @@ def tile_list_freezedry_deviation_match_kernel(
         minima(0)
         quantise_w2(0, 1, nc.scalar.copy)
         maxima(0)
-        features(0, 0, 0, JT // 2)
-        features(0, 0, JT // 2, JT)
+        features(0, 0, bank[0], 0, JT // 2, minima_first=True)
+        features(0, 0, bank[1], JT // 2, JT, minima_first=True)
         for t in range(1, PACK):
-            features(0, t)
+            features(0, t, bank[8 - t])
         put(0, 0, 0, JT // 2)
         put(0, 0, JT // 2, JT)
-        pick_classes(0, 0)
-        pick_runs(0, 0, 0, NP)
-        put_and_pick_classes(0, 1)
-        pick_runs(0, 1, 0, NP)
+        put(0, 1)
+        for t in (0, 1):
+            pick_classes(0, t)
+            pick_runs(0, t, 0, NP)
         minima(1)
         for a in range(KP):
             quantise_w2(1, a, nc.scalar.copy)
         put_and_pick_classes(0, 2)
-        pick_runs(0, 2, 0, NP)
         for t in (0, 1, 2):
             finish_classes(0, t)
         maxima(1)
-        put_and_pick_classes(0, 3)
+        put(0, 3)
+        pick_runs(0, 2, 0, NP)
+        pick_classes(0, 3)
         pick_runs(0, 3, 0, NP)
         for t in range(PACK):
-            features(1, t)
+            features(1, t, bank[t])
         finish_classes(0, 3)
 
-        x1_planes.append(tile([P, PACK, NP], BF16, "x1_planes1", tag="wg_rest"))
-        mat_t = tile([P, MT, NP], F32, "mat_t", tag="w2_raw00")
-        result = tile([P, MT, NP], F32, "result", tag="w2_raw01")
+        x1_planes[1, 0] = tile([P, PACK, 2 * P], BF16, "x1_planes10", tag="wg_rest")
+        x1_planes[1, 2 * P] = tile([P, PACK, P], BF16, "x1_planes12", tag="h3")
+        mat_t = tile([P, MT, NP], F32, "mat_t", tag="w2_raw00_0")
+        result = tile([P, MT, NP], F32, "result", tag="w2_raw10_0")
         with nc.allow_non_contiguous_dma(reason="one value a partition"):
             nc.sync.dma_start(out=rv_t[:], in_=rv.rearrange("(m p) -> p m", p=P))
         nc.sync.dma_start(out=mat_t[:], in_=mat.rearrange("(m p) j -> p m j", p=P))
@@ -281,7 +301,10 @@ def tile_list_freezedry_deviation_match_kernel(
         for t in range(1, PACK):
             put_and_pick_classes(1, t)
             finish_classes(1, t)
-        chunks = [(0, 2), (2, 3), (3, 4)]
+        chunks = CHUNKS
+        early_runs = tile([P, 3 * P, PACK], BF16, "x1_bf1_early", tag="shifted")
+        x1_bf[1, 0], x1_bf[1, 2 * P] = early_runs[:, : 2 * P, :], early_runs[:, 2 * P :, :]
+        x1_bf[1, 3 * P] = tile([P, P, PACK], BF16, "x1_bf1_last")
 
         def pick_chunk(m0, m1):
             for t in range(PACK):
@@ -289,7 +312,7 @@ def tile_list_freezedry_deviation_match_kernel(
 
         def finish(m):
             nc.vector.scalar_tensor_tensor(
-                out=result[:, m, :], in0=bank[m][:], scalar=rv_t[:, m : m + 1], in1=mat_t[:, m, :],
+                out=result[:, m, :], in0=bank[4 + m][:], scalar=rv_t[:, m : m + 1], in1=mat_t[:, m, :],
                 op0=ALU.add, op1=ALU.mult,
             )
             nc.sync.dma_start(out=out[P * m : P * (m + 1), :], in_=result[:, m, :])
@@ -303,6 +326,7 @@ def tile_list_freezedry_deviation_match_kernel(
         quantise_classes(1)
         pick_chunk(*chunks[1])
         match_chunk(*chunks[0])
+        x1_planes[1, 3 * P] = tile([P, PACK, P], BF16, "x1_planes13", tag="wg_rest")
         pick_chunk(*chunks[2])
         match_chunk(*chunks[1])
         match_chunk(*chunks[2])

@@ -82,7 +82,7 @@ def tile_list_freezedry_deviation_match_kernel(
         wg = [tile([P, S], F32, "wg0"), tile([P, S], F32, "wg1"), tile([P, 2, S], F32, "wg_rest")]
         picked = {(b, t): tile([P, NP], F32, "picked%d%d" % (b, t)) for b in range(HP) for t in range(PACK)}
         shifted = tile([P, NP], F32, "shifted")
-        x1_planes = {(0, 0): tile([P, PACK, NP], BF16, "x1_planes0")}
+        x1_planes = {(0, 0): tile([P, PACK, NP], F32, "x1_planes0")}
         x1_bf = {(0, 0): tile([P, NP, PACK], BF16, "x1_bf0")}
         x2_bf = [tile([P, NP, PACK], BF16, "x2_bf%d" % b) for b in range(HP)]
         x1_w = [tile([P, NP], U32, "x1_w%d" % b) for b in range(HP)]
@@ -137,8 +137,8 @@ def tile_list_freezedry_deviation_match_kernel(
         nc.sync.dma_start(lists["offs"][:], offs)
         load_table(0)
         load_scales(tab_s, tab_scales)
-        load_w1(0)
         load_table(1)
+        load_w1(0)
         load_scales(w1_s[0], w1_scales[:, :, :PASS])
         load_w2(0, 0)
         load_w3(0)
@@ -281,11 +281,11 @@ def tile_list_freezedry_deviation_match_kernel(
         pick_classes(0, 3)
         pick_runs(0, 3, 0, NP)
         for t in range(PACK):
-            features(1, t, bank[t])
+            features(1, t, bank[t], minima_first=(t == 0))
         finish_classes(0, 3)
 
-        x1_planes[1, 0] = tile([P, PACK, 2 * P], BF16, "x1_planes10", tag="wg_rest")
-        x1_planes[1, 2 * P] = tile([P, PACK, P], BF16, "x1_planes12", tag="h3")
+        x1_planes[1, 0] = tile([P, PACK, 2 * P], F32, "x1_planes10", tag="wg_rest")
+        x1_planes[1, 2 * P] = tile([P, PACK, P], F32, "x1_planes12", tag="h3")
         mat_t = tile([P, MT, NP], F32, "mat_t", tag="w2_raw00_0")
         result = tile([P, MT, NP], F32, "result", tag="w2_raw10_0")
         with nc.allow_non_contiguous_dma(reason="one value a partition"):
@@ -310,12 +310,12 @@ def tile_list_freezedry_deviation_match_kernel(
             for t in range(PACK):
                 pick_runs(1, t, P * m0, P * m1)
 
-        def finish(m):
+        def finish(m, cols):
             nc.vector.scalar_tensor_tensor(
-                out=result[:, m, :], in0=bank[4 + m][:], scalar=rv_t[:, m : m + 1], in1=mat_t[:, m, :],
+                out=result[:, m, cols], in0=bank[4 + m][:, cols], scalar=rv_t[:, m : m + 1], in1=mat_t[:, m, cols],
                 op0=ALU.add, op1=ALU.mult,
             )
-            nc.sync.dma_start(out=out[P * m : P * (m + 1), :], in_=result[:, m, :])
+            nc.sync.dma_start(out=out[P * m : P * (m + 1), cols], in_=result[:, m, cols])
 
         def match_chunk(m0, m1):
             quantise_runs(1, P * m0, P * m1)
@@ -326,9 +326,11 @@ def tile_list_freezedry_deviation_match_kernel(
         quantise_classes(1)
         pick_chunk(*chunks[1])
         match_chunk(*chunks[0])
-        x1_planes[1, 3 * P] = tile([P, PACK, P], BF16, "x1_planes13", tag="wg_rest")
+        x1_planes[1, 3 * P] = tile([P, PACK, P], F32, "x1_planes13", tag="wg_rest")
         pick_chunk(*chunks[2])
         match_chunk(*chunks[1])
         match_chunk(*chunks[2])
-        for m in range(MT):
-            finish(m)
+        for m in range(MT - 1):
+            finish(m, slice(0, NP))
+        finish(MT - 1, slice(0, NP // 2))
+        finish(MT - 1, slice(NP // 2, NP))

@@ -134,8 +134,8 @@ def tile_list_freezedry_deviation_match_kernel(
         for b in range(HP):
             nc.vector.memset(w1_s[b][:].bitcast(I32), 0)
             nc.vector.memset(w3_s[b][:].bitcast(I32), 0)
-        nc.sync.dma_start(lists["offs"][:], offs)
         load_table(0)
+        nc.sync.dma_start(lists["offs"][:], offs)
         load_scales(tab_s, tab_scales)
         load_table(1)
         load_w1(0)
@@ -145,12 +145,12 @@ def tile_list_freezedry_deviation_match_kernel(
         load_scales(w3_s[0], w3_scales[:, :, :PASS])
         load_w2(0, 1)
         load_page(0, 0)
-        nc.sync.dma_start(lists["offs2"][:], offs2)
         for q in range(QUAD):
             nc.sync.dma_start(out=wg[0][32 * q : 32 * (q + 1), :], in_=wgs_rows[:, 0, :])
         for q in range(QUAD):
             nc.sync.dma_start(out=wg[1][32 * q : 32 * (q + 1), :], in_=wgs_rows[:, 1, :])
         load_page(0, 1)
+        nc.sync.dma_start(lists["offs2"][:], offs2)
         nc.sync.dma_start(lists["offs4"][:], offs4)
         nc.sync.dma_start(lists["offs3"][:], offs3)
         load_w1(1)
@@ -222,16 +222,25 @@ def tile_list_freezedry_deviation_match_kernel(
             entries = lists["offs2"][:, P * j0 // 16 : P * j1 // 16]
             nc.vector.tensor_tensor(page[b, t][:].indirect(entries), h[b, t][:, cols], wgs_plane(t)[:, cols], ALU.mult)
 
-        def pick_classes(b, t):
-            nc.vector.tensor_copy(picked[b, t][:], page[b, t][:].indirect(lists["offs4"][:]))
+        def pick_classes(b, t, c0=0, c1=NP):
+            nc.vector.tensor_copy(picked[b, t][:, c0:c1], page[b, t][:].indirect(lists["offs4"][:, c0 // 16 : c1 // 16]))
 
         def put_and_pick_classes(b, t):
             put(b, t)
             pick_classes(b, t)
 
-        def finish_classes(b, t):
-            nc.scalar.activation(out=shifted[:], in_=picked[b, t][:], func=ACT.Identity, bias=bd_t[:, b, t : t + 1], scale=1.0)
-            nc.scalar.activation(out=x2_bf[b][:, :, t], in_=shifted[:], func=ACT.Copy, scale=gd_t[:, b, t : t + 1])
+        def finish_classes(b, t, parts=1):
+            width = NP // parts
+            for c in range(0, NP, width):
+                nc.scalar.activation(
+                    out=shifted[:, c : c + width], in_=picked[b, t][:, c : c + width], func=ACT.Identity,
+                    bias=bd_t[:, b, t : t + 1], scale=1.0,
+                )
+            for c in range(0, NP, width):
+                nc.scalar.activation(
+                    out=x2_bf[b][:, c : c + width, t], in_=shifted[:, c : c + width], func=ACT.Copy,
+                    scale=gd_t[:, b, t : t + 1],
+                )
 
         def pick_runs(b, t, m0, m1):
             nc.vector.tensor_copy(x1_planes[b, m0][:, t, :], page[b, t][:].indirect(lists["offs3"][:, m0 // 16 : m1 // 16]))
@@ -259,13 +268,15 @@ def tile_list_freezedry_deviation_match_kernel(
         minima(0)
         quantise_w2(0, 1, nc.scalar.copy)
         maxima(0)
-        features(0, 0, bank[0], 0, JT // 2, minima_first=True)
-        features(0, 0, bank[1], JT // 2, JT, minima_first=True)
-        for t in range(1, PACK):
-            features(0, t, bank[8 - t])
-        put(0, 0, 0, JT // 2)
-        put(0, 0, JT // 2, JT)
-        put(0, 1)
+        halves = ((0, JT // 2), (JT // 2, JT))
+        for i, (j0, j1) in enumerate(halves):
+            for t in (0, 1):
+                features(0, t, bank[2 * i + t], j0, j1, minima_first=True)
+        for t in (2, 3):
+            features(0, t, bank[9 - t])
+        for j0, j1 in halves:
+            for t in (0, 1):
+                put(0, t, j0, j1)
         for t in (0, 1):
             pick_classes(0, t)
             pick_runs(0, t, 0, NP)
@@ -280,7 +291,7 @@ def tile_list_freezedry_deviation_match_kernel(
         pick_runs(0, 2, 0, NP)
         pick_classes(0, 3)
         pick_runs(0, 3, 0, NP)
-        for t in range(PACK):
+        for t in range(PACK - 1):
             features(1, t, bank[t], minima_first=(t == 0))
         finish_classes(0, 3)
 
@@ -294,13 +305,18 @@ def tile_list_freezedry_deviation_match_kernel(
 
         put_and_pick_classes(1, 0)
         quantise_runs(0, 0, NP)
+        features(1, PACK - 1, bank[PACK - 1])
         finish_classes(1, 0)
         quantise_classes(0)
         for m in range(MT):
             match(0, m)
-        for t in range(1, PACK):
+        for t in range(1, PACK - 1):
             put_and_pick_classes(1, t)
             finish_classes(1, t)
+        put(1, PACK - 1)
+        pick_classes(1, PACK - 1, 0, NP // 2)
+        pick_classes(1, PACK - 1, NP // 2, NP)
+        finish_classes(1, PACK - 1, parts=2)
         chunks = CHUNKS
         early_runs = tile([P, 3 * P, PACK], BF16, "x1_bf1_early", tag="shifted")
         x1_bf[1, 0], x1_bf[1, 2 * P] = early_runs[:, : 2 * P, :], early_runs[:, 2 * P :, :]

@@ -20,12 +20,13 @@ ACT = mybir.ActivationFunctionType
 P = 128
 PACK = 4
 PASS = P * PACK
-KP = K // PASS
-HP = H // PASS
-JT = S // P
-MT = NP // P
-QUAD = 4
-CHUNKS = ((0, 2), (2, 3), (3, 4))
+K_PASSES = K // PASS
+HALVES = H // PASS
+J_TILES = S // P
+M_TILES = NP // P
+QUADRANTS = 4
+LIST_ROWS = 16
+UPPER = 4
 
 
 def interleave(copy, dst, src):
@@ -33,6 +34,14 @@ def interleave(copy, dst, src):
         out=dst.rearrange("p (c i) t -> p c t i", i=4),
         in_=src.rearrange("p t (c i) -> p c t i", i=4),
     )
+
+
+def by_word_pairs(bank):
+    return bank[:].rearrange("p (q s e) -> p s q e", s=2, e=2)
+
+
+def as_pair_planes(flat):
+    return flat[:].rearrange("p (s q e) -> p s q e", s=2, e=2)
 
 
 def tile_list_freezedry_deviation_match_kernel(
@@ -44,61 +53,69 @@ def tile_list_freezedry_deviation_match_kernel(
         keep = ctx.enter_context(tc.tile_pool(name="keep", bufs=1))
         psum = ctx.enter_context(tc.psum_pool(name="psum", bufs=1))
 
-        def tile(shape, dtype, name, tag=None):
-            return keep.tile(shape, dtype, name=name, tag=tag or name, align_bytes=64)
+        def tile(shape, dtype, name, after=None):
+            return keep.tile(shape, dtype, name=name, tag=after or name, align_bytes=64)
 
         lists = {}
         for name in ("offs", "offs2", "offs3", "offs4"):
-            lists[name] = tile([P, S // 16], U16, "list_" + name)
-        bank = [psum.tile([P, PASS], F32, name="bank%d" % i) for i in range(8)]
+            lists[name] = tile([P, S // LIST_ROWS], U16, "list_" + name)
+        bank = [psum.tile([P, PASS], F32, name="bank%d" % i) for i in range(2 * UPPER)]
 
-        tab_w = [tile([P, T], U32, "tab_w%d" % a) for a in range(KP)]
-        tab_s = tile([P, KP, T], U8, "tab_s")
-        v_w = [tile([P, S], U32, "v_w%d" % a) for a in range(KP)]
-        v_s = [tile([P, S], U8, "v_s%d" % a) for a in range(KP)]
-        w1_w = [tile([P, KP, 2 * PASS], U8, "w1_w%d" % b) for b in range(HP)]
-        w3_w = [tile([P, KP, PASS], U32, "w3_w%d" % b) for b in range(HP)]
-        w1_s = [tile([P, KP, PASS], U8, "w1_s%d" % b) for b in range(HP)]
-        w3_s = [tile([P, KP, PASS], U8, "w3_s%d" % b) for b in range(HP)]
+        tab_w = [tile([P, T], U32, "tab_w%d" % a) for a in range(K_PASSES)]
+        tab_s = tile([P, K_PASSES, T], U8, "tab_s")
+        v_w = [tile([P, S], U32, "v_w%d" % a) for a in range(K_PASSES)]
+        v_s = [tile([P, S], U8, "v_s%d" % a) for a in range(K_PASSES)]
+        w1_w = [tile([P, K_PASSES, 2 * PASS], U8, "w1_w%d" % b) for b in range(HALVES)]
+        w3_w = [tile([P, K_PASSES, PASS], U32, "w3_w%d" % b) for b in range(HALVES)]
+        w1_s = [tile([P, K_PASSES, PASS], U8, "w1_s%d" % b) for b in range(HALVES)]
+        w3_s = [tile([P, K_PASSES, PASS], U8, "w3_s%d" % b) for b in range(HALVES)]
         w2_raw = {}
-        for b in range(HP):
-            for a in range(KP):
-                width = PASS // 2 if (b, a) == (0, KP - 1) else PASS
+        for b in range(HALVES):
+            for a in range(K_PASSES):
+                width = PASS // 2 if (b, a) == (0, K_PASSES - 1) else PASS
                 w2_raw[b, a] = [
                     (slice(c, c + width), tile([P, PACK, width], F32, "w2_raw%d%d_%d" % (b, a, c)))
                     for c in range(0, PASS, width)
                 ]
-        w2_bf = [tile([P, PASS, PACK], BF16, "w2_bf%d" % a) for a in range(KP)]
-        w2_w = {(b, a): tile([P, PASS], U32, "w2_w%d%d" % (b, a)) for b in range(HP) for a in range(KP)}
-        w2_s = {(b, a): tile([P, PASS], U8, "w2_s%d%d" % (b, a)) for b in range(HP) for a in range(KP)}
-        y1 = [tile([P, 2, P, 2], F32, "y1_%d" % j) for j in range(JT)]
-        low = [tile([P, 2, P, 2], F32, "low%d" % j)[:] for j in range(JT)]
-        high = {(0, j): tile([P, S], F32, "high%d" % j) for j in range(JT)}
+        w2_bf = [tile([P, PASS, PACK], BF16, "w2_bf%d" % a) for a in range(K_PASSES)]
+        w2_w = {(b, a): tile([P, PASS], U32, "w2_w%d%d" % (b, a)) for b in range(HALVES) for a in range(K_PASSES)}
+        w2_s = {(b, a): tile([P, PASS], U8, "w2_s%d%d" % (b, a)) for b in range(HALVES) for a in range(K_PASSES)}
+
+        y1 = [tile([P, 2, P, 2], F32, "y1_%d" % j) for j in range(J_TILES)]
+        low = [tile([P, 2, P, 2], F32, "low%d" % j)[:] for j in range(J_TILES)]
+        high = {(0, j): tile([P, S], F32, "high%d" % j) for j in range(J_TILES)}
         h = {(0, t): tile([P, S], F32, "h%d" % t) for t in range(PACK)}
         for i in range(PACK):
             high[1, i], h[1, i] = high[0, i], h[0, i]
         high[1, 0], h[1, 2] = h[0, 2], high[0, 0]
-        page = {(b, t): tile([P, T2], F32, "page%d%d" % (b, t)) for b in range(HP) for t in range(PACK)}
-        wg = [tile([P, S], F32, "wg0"), tile([P, S], F32, "wg1"), tile([P, 2, S], F32, "wg_rest")]
-        picked = {(b, t): tile([P, NP], F32, "picked%d%d" % (b, t)) for b in range(HP) for t in range(PACK)}
+
+        page = {(b, t): tile([P, T2], F32, "page%d%d" % (b, t)) for b in range(HALVES) for t in range(PACK)}
+        wg = [tile([P, S], F32, "wg0"), tile([P, S], F32, "wg1"), tile([P, 2, S], F32, "wg23")]
+        picked = {(b, t): tile([P, NP], F32, "picked%d%d" % (b, t)) for b in range(HALVES) for t in range(PACK)}
         shifted = tile([P, NP], F32, "shifted")
         x1_planes = {(0, 0): tile([P, PACK, NP], F32, "x1_planes0")}
         x1_bf = {(0, 0): tile([P, NP, PACK], BF16, "x1_bf0")}
-        x2_bf = [tile([P, NP, PACK], BF16, "x2_bf%d" % b) for b in range(HP)]
-        x1_w = [tile([P, NP], U32, "x1_w%d" % b) for b in range(HP)]
-        x2_w = [tile([P, NP], U32, "x2_w%d" % b) for b in range(HP)]
-        x1_s = [tile([P, NP], U8, "x1_s%d" % b) for b in range(HP)]
-        x2_s = [tile([P, NP], U8, "x2_s%d" % b) for b in range(HP)]
-        bd_t = tile([P, HP, PACK], F32, "bd_t")
-        gd_t = tile([P, HP, PACK], F32, "gd_t")
-        rv_t = tile([P, MT], F32, "rv_t")
+        x2_bf = [tile([P, NP, PACK], BF16, "x2_bf%d" % b) for b in range(HALVES)]
+        x1_w = {}
+        x1_w_second_half = tile([P, NP], U32, "x1_w1")
+        for m in range(M_TILES):
+            x1_w[1, m] = x1_w_second_half[:, P * m :]
+        x2_w = [tile([P, NP], U32, "x2_w%d" % b) for b in range(HALVES)]
+        x1_s = [tile([P, NP], U8, "x1_s%d" % b) for b in range(HALVES)]
+        x2_s = [tile([P, NP], U8, "x2_s%d" % b) for b in range(HALVES)]
+        bd_t = tile([P, HALVES, PACK], F32, "bd_t")
+        gd_t = tile([P, HALVES, PACK], F32, "gd_t")
+        rv_t = tile([P, M_TILES], F32, "rv_t")
         ident = tile([P, P], F32, "ident")
 
-        def wgs_plane(t):
+        def wgs_rows_of_slot(t):
             return wg[t][:] if t < 2 else wg[2][:, t - 2, :]
 
+        def load_list(name, src):
+            nc.sync.dma_start(lists[name][:], src)
+
         def load_scales(dst, src):
-            for q in range(QUAD):
+            for q in range(QUADRANTS):
                 nc.sync.dma_start(
                     out=dst[32 * q : 32 * q + 4, :, :].bitcast(I32),
                     in_=src[:, 4 * q : 4 * q + 4, :].rearrange("a r c -> r a c").bitcast(I32),
@@ -112,12 +129,14 @@ def tile_list_freezedry_deviation_match_kernel(
                 out=w1_w[b][:].bitcast(I32),
                 in_=w1_words[:, :, 2 * PASS * b : 2 * PASS * (b + 1)].rearrange("a p c -> p a c").bitcast(I32),
             )
+            load_scales(w1_s[b], w1_scales[:, :, PASS * b : PASS * (b + 1)])
 
         def load_w3(b):
             nc.sync.dma_start(
                 out=w3_w[b][:].bitcast(I32),
                 in_=w3_words[:, :, PASS * b : PASS * (b + 1), :].rearrange("a p c i -> p a (c i)").bitcast(I32),
             )
+            load_scales(w3_s[b], w3_scales[:, :, PASS * b : PASS * (b + 1)])
 
         def load_w2(b, a):
             rows = w2[PASS * a : PASS * (a + 1), PASS * b : PASS * (b + 1)].rearrange("(p i) c -> p i c", i=PACK)
@@ -128,69 +147,63 @@ def tile_list_freezedry_deviation_match_kernel(
             rows = page0[PASS * b : PASS * (b + 1), :].rearrange("(p t) c -> p t c", t=PACK)
             nc.sync.dma_start(out=page[b, t][:], in_=rows[:, t, :])
 
-        wgs_rows = wgs.rearrange("(q t) c -> q t c", t=PACK)
+        def load_wgs(dst, slots):
+            rows = wgs.rearrange("(q t) c -> q t c", t=PACK)
+            for q in range(QUADRANTS):
+                nc.sync.dma_start(out=dst[32 * q : 32 * (q + 1)], in_=rows[:, slots, :])
 
         nc.vector.memset(tab_s[:].bitcast(I32), 0)
-        for b in range(HP):
+        for b in range(HALVES):
             nc.vector.memset(w1_s[b][:].bitcast(I32), 0)
             nc.vector.memset(w3_s[b][:].bitcast(I32), 0)
+
         load_table(0)
-        nc.sync.dma_start(lists["offs"][:], offs)
+        load_list("offs", offs)
         load_scales(tab_s, tab_scales)
         load_table(1)
         load_w1(0)
-        load_scales(w1_s[0], w1_scales[:, :, :PASS])
         load_w2(0, 0)
         load_w3(0)
-        load_scales(w3_s[0], w3_scales[:, :, :PASS])
         load_w2(0, 1)
         load_page(0, 0)
-        for q in range(QUAD):
-            nc.sync.dma_start(out=wg[0][32 * q : 32 * (q + 1), :], in_=wgs_rows[:, 0, :])
-        for q in range(QUAD):
-            nc.sync.dma_start(out=wg[1][32 * q : 32 * (q + 1), :], in_=wgs_rows[:, 1, :])
+        load_wgs(wg[0], 0)
+        load_wgs(wg[1], 1)
         load_page(0, 1)
-        nc.sync.dma_start(lists["offs2"][:], offs2)
-        nc.sync.dma_start(lists["offs4"][:], offs4)
-        nc.sync.dma_start(lists["offs3"][:], offs3)
+        load_list("offs2", offs2)
+        load_list("offs4", offs4)
+        load_list("offs3", offs3)
         load_w1(1)
-        load_scales(w1_s[1], w1_scales[:, :, PASS:])
         load_w3(1)
-        load_scales(w3_s[1], w3_scales[:, :, PASS:])
-        for q in range(QUAD):
-            nc.sync.dma_start(out=wg[2][32 * q : 32 * (q + 1), :, :], in_=wgs_rows[:, 2:PACK, :])
+        load_wgs(wg[2], slice(2, PACK))
         load_w2(1, 0)
         load_w2(1, 1)
-        nc.sync.dma_start(out=bd_t[:], in_=bd.rearrange("(b p t) -> p b t", b=HP, t=PACK))
-        nc.sync.dma_start(out=gd_t[:], in_=gd.rearrange("(b p t) -> p b t", b=HP, t=PACK))
-        for b, t in ((1, 0), (0, 2), (1, 1), (0, 3), (1, 2), (1, 3)):
-            load_page(b, t)
+        nc.sync.dma_start(out=bd_t[:], in_=bd.rearrange("(b p t) -> p b t", b=HALVES, t=PACK))
+        nc.sync.dma_start(out=gd_t[:], in_=gd.rearrange("(b p t) -> p b t", b=HALVES, t=PACK))
+        for t in range(2):
+            load_page(1, t)
+            load_page(0, 2 + t)
+        for t in range(2, PACK):
+            load_page(1, t)
         make_identity(nc, ident[:])
 
-        for a in range(KP):
+        for a in range(K_PASSES):
             nc.vector.tensor_copy(v_w[a][:], tab_w[a][:].indirect(lists["offs"][:]))
             nc.vector.tensor_copy(v_s[a][:], tab_s[:, a, :].indirect(lists["offs"][:]))
 
-        def first_stage(dst, j, rhs, rhs_scale):
+        def first_stage(acc, j, words, scales):
             cols = slice(P * j, P * (j + 1))
-            for a in range(KP):
+            for a in range(K_PASSES):
                 nc.tensor.matmul_mx(
-                    out=dst[:], lhsT=v_w[a][:, cols].bitcast(FP8X4), lhsT_scale=v_s[a][:, cols],
-                    rhs=rhs(a), rhs_scale=rhs_scale(a), start=(a == 0), stop=(a == KP - 1),
+                    out=acc[:], lhsT=v_w[a][:, cols].bitcast(FP8X4), lhsT_scale=v_s[a][:, cols],
+                    rhs=words(a), rhs_scale=scales(a), start=(a == 0), stop=(a == K_PASSES - 1),
                 )
 
-        def dealt(b_):
-            return b_[:].rearrange("p (q s e) -> p s q e", s=2, e=2)
-
-        def planes(flat):
-            return flat[:].rearrange("p (s q e) -> p s q e", s=2, e=2)
-
         def minima(b):
-            for j in range(JT):
+            for j in range(J_TILES):
                 first_stage(bank[j], j, lambda a: w1_w[b][:, a, :].bitcast(FP4X4), lambda a: w1_s[b][:, a, :])
-                first_stage(bank[4 + j], j, lambda a: w3_w[b][:, a, :].bitcast(FP8X4), lambda a: w3_s[b][:, a, :])
-                nc.scalar.copy(out=y1[j][:], in_=dealt(bank[j]))
-                nc.vector.tensor_tensor(low[j], dealt(bank[4 + j]), y1[j][:], ALU.min)
+                first_stage(bank[UPPER + j], j, lambda a: w3_w[b][:, a, :].bitcast(FP8X4), lambda a: w3_s[b][:, a, :])
+                nc.scalar.copy(out=y1[j][:], in_=by_word_pairs(bank[j]))
+                nc.vector.tensor_tensor(low[j], by_word_pairs(bank[UPPER + j]), y1[j][:], ALU.min)
 
         def quantise_w2(b, a, copy):
             for cols, raw in w2_raw[b, a]:
@@ -201,15 +214,15 @@ def tile_list_freezedry_deviation_match_kernel(
             )
 
         def maxima(b):
-            for j in range(JT):
-                first_stage(bank[4 + j], j, lambda a: w2_w[b, a][:].bitcast(FP8X4), lambda a: w2_s[b, a][:])
-                nc.vector.tensor_tensor(planes(high[b, j]), dealt(bank[4 + j]), y1[j][:], ALU.max)
+            for j in range(J_TILES):
+                first_stage(bank[UPPER + j], j, lambda a: w2_w[b, a][:].bitcast(FP8X4), lambda a: w2_s[b, a][:])
+                nc.vector.tensor_tensor(as_pair_planes(high[b, j]), by_word_pairs(bank[UPPER + j]), y1[j][:], ALU.max)
 
-        def features(b, t, acc, j0=0, j1=JT, minima_first=False):
+        def features(b, t, acc, j0=0, j1=J_TILES, minima_first=False):
             if minima_first:
-                terms = [(low[j], j) for j in range(j0, j1)] + [(planes(high[b, j]), j) for j in range(j0, j1)]
+                terms = [(low[j], j) for j in range(j0, j1)] + [(as_pair_planes(high[b, j]), j) for j in range(j0, j1)]
             else:
-                terms = [(term, j) for j in range(j0, j1) for term in (planes(high[b, j]), low[j])]
+                terms = [(term, j) for j in range(j0, j1) for term in (as_pair_planes(high[b, j]), low[j])]
             for n, (term, j) in enumerate(terms):
                 nc.tensor.matmul(
                     out=acc[:, P * j : P * (j + 1)], lhsT=term[:, t // 2, :, t % 2], rhs=ident[:],
@@ -217,17 +230,14 @@ def tile_list_freezedry_deviation_match_kernel(
                 )
             nc.scalar.copy(out=h[b, t][:, P * j0 : P * j1], in_=acc[:, P * j0 : P * j1])
 
-        def put(b, t, j0=0, j1=JT):
+        def put(b, t, j0=0, j1=J_TILES):
             cols = slice(P * j0, P * j1)
-            entries = lists["offs2"][:, P * j0 // 16 : P * j1 // 16]
-            nc.vector.tensor_tensor(page[b, t][:].indirect(entries), h[b, t][:, cols], wgs_plane(t)[:, cols], ALU.mult)
+            entries = lists["offs2"][:, P * j0 // LIST_ROWS : P * j1 // LIST_ROWS]
+            nc.vector.tensor_tensor(page[b, t][:].indirect(entries), h[b, t][:, cols], wgs_rows_of_slot(t)[:, cols], ALU.mult)
 
         def pick_classes(b, t, c0=0, c1=NP):
-            nc.vector.tensor_copy(picked[b, t][:, c0:c1], page[b, t][:].indirect(lists["offs4"][:, c0 // 16 : c1 // 16]))
-
-        def put_and_pick_classes(b, t):
-            put(b, t)
-            pick_classes(b, t)
+            entries = lists["offs4"][:, c0 // LIST_ROWS : c1 // LIST_ROWS]
+            nc.vector.tensor_copy(picked[b, t][:, c0:c1], page[b, t][:].indirect(entries))
 
         def finish_classes(b, t, parts=1):
             width = NP // parts
@@ -243,13 +253,16 @@ def tile_list_freezedry_deviation_match_kernel(
                 )
 
         def pick_runs(b, t, m0, m1):
-            nc.vector.tensor_copy(x1_planes[b, m0][:, t, :], page[b, t][:].indirect(lists["offs3"][:, m0 // 16 : m1 // 16]))
+            entries = lists["offs3"][:, m0 // LIST_ROWS : m1 // LIST_ROWS]
+            nc.vector.tensor_copy(x1_planes[b, m0][:, t, :], page[b, t][:].indirect(entries))
 
-        def quantise_runs(b, m0, m1):
+        def round_runs(b, m0):
             interleave(nc.scalar.copy, x1_bf[b, m0][:], x1_planes[b, m0][:])
+
+        def quantise_runs(b, m0, m1, rounded):
             nc.vector.quantize_mx(
-                out=x1_w[b][:, m0:m1].bitcast(FP8X4), scales=x1_s[b][:, m0:m1],
-                in_=x1_bf[b, m0][:].rearrange("p c i -> p (c i)"),
+                out=x1_w[b, m0 // P][:, : m1 - m0].bitcast(FP8X4), scales=x1_s[b][:, m0:m1],
+                in_=rounded.rearrange("p c i -> p (c i)"),
             )
 
         def quantise_classes(b):
@@ -260,31 +273,33 @@ def tile_list_freezedry_deviation_match_kernel(
         def match(b, m):
             cols = slice(P * m, P * (m + 1))
             nc.tensor.matmul_mx(
-                out=bank[4 + m][:], lhsT=x1_w[b][:, cols].bitcast(FP8X4), lhsT_scale=x1_s[b][:, cols],
-                rhs=x2_w[b][:].bitcast(FP8X4), rhs_scale=x2_s[b][:], start=(b == 0), stop=(b == HP - 1),
+                out=bank[UPPER + m][:], lhsT=x1_w[b, m][:, :P].bitcast(FP8X4), lhsT_scale=x1_s[b][:, cols],
+                rhs=x2_w[b][:].bitcast(FP8X4), rhs_scale=x2_s[b][:], start=(b == 0), stop=(b == HALVES - 1),
             )
 
         quantise_w2(0, 0, nc.vector.tensor_copy)
         minima(0)
         quantise_w2(0, 1, nc.scalar.copy)
         maxima(0)
-        halves = ((0, JT // 2), (JT // 2, JT))
-        for i, (j0, j1) in enumerate(halves):
-            for t in (0, 1):
-                features(0, t, bank[2 * i + t], j0, j1, minima_first=True)
-        for t in (2, 3):
-            features(0, t, bank[9 - t])
-        for j0, j1 in halves:
-            for t in (0, 1):
+        entry_parts = ((0, J_TILES // 2), (J_TILES // 2, J_TILES))
+        for i, (j0, j1) in enumerate(entry_parts):
+            for t in range(2):
+                features(0, t, bank[2 * i + t], j0, j1, minima_first=(i == 0))
+        features(0, 2, bank[UPPER + 3])
+        features(0, 3, bank[UPPER + 2])
+        for j0, j1 in entry_parts:
+            for t in range(2):
                 put(0, t, j0, j1)
-        for t in (0, 1):
+        for t in range(2):
             pick_classes(0, t)
             pick_runs(0, t, 0, NP)
+
         minima(1)
-        for a in range(KP):
+        for a in range(K_PASSES):
             quantise_w2(1, a, nc.scalar.copy)
-        put_and_pick_classes(0, 2)
-        for t in (0, 1, 2):
+        put(0, 2)
+        pick_classes(0, 2)
+        for t in range(PACK - 1):
             finish_classes(0, t)
         maxima(1)
         put(0, 3)
@@ -295,30 +310,36 @@ def tile_list_freezedry_deviation_match_kernel(
             features(1, t, bank[t], minima_first=(t == 0))
         finish_classes(0, 3)
 
-        x1_planes[1, 0] = tile([P, PACK, 2 * P], F32, "x1_planes10", tag="wg_rest")
-        x1_planes[1, 2 * P] = tile([P, PACK, P], F32, "x1_planes12", tag="h3")
-        mat_t = tile([P, MT, NP], F32, "mat_t", tag="w2_raw00_0")
-        result = tile([P, MT, NP], F32, "result", tag="w2_raw10_0")
+        x1_planes[1, 0] = tile([P, PACK, 2 * P], F32, "x1_planes10", after="wg23")
+        x1_planes[1, 2 * P] = tile([P, PACK, P], F32, "x1_planes12", after="h3")
+        mat_t = tile([P, M_TILES, NP], F32, "mat_t", after="w2_raw00_0")
+        result = tile([P, M_TILES, NP], F32, "result", after="w2_raw10_0")
         with nc.allow_non_contiguous_dma(reason="one value a partition"):
             nc.sync.dma_start(out=rv_t[:], in_=rv.rearrange("(m p) -> p m", p=P))
         nc.sync.dma_start(out=mat_t[:], in_=mat.rearrange("(m p) j -> p m j", p=P))
 
-        put_and_pick_classes(1, 0)
-        quantise_runs(0, 0, NP)
-        features(1, PACK - 1, bank[PACK - 1])
+        put(1, 0)
+        pick_classes(1, 0)
+        round_runs(0, 0)
+        features(1, 3, bank[3])
         finish_classes(1, 0)
         quantise_classes(0)
-        for m in range(MT):
-            match(0, m)
         for t in range(1, PACK - 1):
-            put_and_pick_classes(1, t)
+            put(1, t)
+            pick_classes(1, t)
             finish_classes(1, t)
-        put(1, PACK - 1)
-        pick_classes(1, PACK - 1, 0, NP // 2)
-        pick_classes(1, PACK - 1, NP // 2, NP)
-        finish_classes(1, PACK - 1, parts=2)
-        chunks = CHUNKS
-        early_runs = tile([P, 3 * P, PACK], BF16, "x1_bf1_early", tag="shifted")
+        put(1, 3)
+        pick_classes(1, 3, 0, NP // 2)
+        pick_classes(1, 3, NP // 2, NP)
+        finish_classes(1, 3, parts=2)
+
+        for i in range(2):
+            words = tile([P, 2 * P], U32, "x1_w0%d" % i, after="picked1%d" % i)
+            x1_w[0, 2 * i], x1_w[0, 2 * i + 1] = words[:], words[:, P:]
+            quantise_runs(0, 2 * P * i, 2 * P * (i + 1), x1_bf[0, 0][:, 2 * P * i : 2 * P * (i + 1), :])
+            match(0, 2 * i)
+            match(0, 2 * i + 1)
+        early_runs = tile([P, 3 * P, PACK], BF16, "x1_bf1_early", after="shifted")
         x1_bf[1, 0], x1_bf[1, 2 * P] = early_runs[:, : 2 * P, :], early_runs[:, 2 * P :, :]
         x1_bf[1, 3 * P] = tile([P, P, PACK], BF16, "x1_bf1_last")
 
@@ -326,27 +347,28 @@ def tile_list_freezedry_deviation_match_kernel(
             for t in range(PACK):
                 pick_runs(1, t, P * m0, P * m1)
 
+        def match_chunk(m0, m1):
+            round_runs(1, P * m0)
+            quantise_runs(1, P * m0, P * m1, x1_bf[1, P * m0][:])
+            for m in range(m0, m1):
+                match(1, m)
+
         def finish(m, cols):
             nc.vector.scalar_tensor_tensor(
-                out=result[:, m, cols], in0=bank[4 + m][:, cols], scalar=rv_t[:, m : m + 1], in1=mat_t[:, m, cols],
+                out=result[:, m, cols], in0=bank[UPPER + m][:, cols], scalar=rv_t[:, m : m + 1], in1=mat_t[:, m, cols],
                 op0=ALU.add, op1=ALU.mult,
             )
             nc.sync.dma_start(out=out[P * m : P * (m + 1), cols], in_=result[:, m, cols])
 
-        def match_chunk(m0, m1):
-            quantise_runs(1, P * m0, P * m1)
-            for m in range(m0, m1):
-                match(1, m)
-
-        pick_chunk(*chunks[0])
+        pick_chunk(0, 2)
         quantise_classes(1)
-        pick_chunk(*chunks[1])
-        match_chunk(*chunks[0])
-        x1_planes[1, 3 * P] = tile([P, PACK, P], F32, "x1_planes13", tag="wg_rest")
-        pick_chunk(*chunks[2])
-        match_chunk(*chunks[1])
-        match_chunk(*chunks[2])
-        for m in range(MT - 1):
+        pick_chunk(2, 3)
+        match_chunk(0, 2)
+        x1_planes[1, 3 * P] = tile([P, PACK, P], F32, "x1_planes13", after="wg23")
+        pick_chunk(3, 4)
+        match_chunk(2, 3)
+        match_chunk(3, 4)
+        for m in range(M_TILES - 1):
             finish(m, slice(0, NP))
-        finish(MT - 1, slice(0, NP // 2))
-        finish(MT - 1, slice(NP // 2, NP))
+        finish(M_TILES - 1, slice(0, NP // 2))
+        finish(M_TILES - 1, slice(NP // 2, NP))

from contextlib import ExitStack

import concourse.mybir as mybir
from concourse.masks import make_identity

K, H, T, S, T2, NP = 1024, 1024, 2048, 512, 1024, 512
FLOPS = 3 * 2 * K * H * S + 2 * H * NP * NP

F32 = mybir.dt.float32
BF16 = mybir.dt.bfloat16
I32 = mybir.dt.int32
U32 = mybir.dt.uint32
U16 = mybir.dt.uint16
U8 = mybir.dt.uint8
FP8X4 = mybir.dt.float8_e4m3fn_x4
FP4X4 = mybir.dt.float4_e2m1fn_x4
ALU = mybir.AluOpType
ACT = mybir.ActivationFunctionType

P = 128
PACK = 4
PASS = P * PACK
K_PASSES = K // PASS
HALVES = H // PASS
J_TILES = S // P
M_TILES = NP // P
QUADRANTS = 4
LIST_ROWS = 16
UPPER = 4


def interleave(copy, dst, src):
    copy(
        out=dst.rearrange("p (c i) t -> p c t i", i=4),
        in_=src.rearrange("p t (c i) -> p c t i", i=4),
    )


def by_word_pairs(bank):
    return bank[:].rearrange("p (q s e) -> p s q e", s=2, e=2)


def as_pair_planes(flat):
    return flat[:].rearrange("p (s q e) -> p s q e", s=2, e=2)


def tile_list_freezedry_deviation_match_kernel(
    tc, tab_words, tab_scales, offs, w1_words, w1_scales, w2, w3_words, w3_scales,
    page0, wgs, offs2, offs3, offs4, bd, gd, rv, mat, out,
):
    nc = tc.nc
    with ExitStack() as ctx:
        keep = ctx.enter_context(tc.tile_pool(name="keep", bufs=1))
        psum = ctx.enter_context(tc.psum_pool(name="psum", bufs=1))

        def tile(shape, dtype, name, after=None):
            return keep.tile(shape, dtype, name=name, tag=after or name, align_bytes=64)

        lists = {}
        for name in ("offs", "offs2", "offs3", "offs4"):
            lists[name] = tile([P, S // LIST_ROWS], U16, "list_" + name)
        bank = [psum.tile([P, PASS], F32, name="bank%d" % i) for i in range(2 * UPPER)]

        tab_w = [tile([P, T], U32, "tab_w%d" % a) for a in range(K_PASSES)]
        tab_s = tile([P, K_PASSES, T], U8, "tab_s")
        v_w = [tile([P, S], U32, "v_w%d" % a) for a in range(K_PASSES)]
        v_s = [tile([P, S], U8, "v_s%d" % a) for a in range(K_PASSES)]
        w1_w = [tile([P, K_PASSES, 2 * PASS], U8, "w1_w%d" % b) for b in range(HALVES)]
        w3_w = [tile([P, K_PASSES, PASS], U32, "w3_w%d" % b) for b in range(HALVES)]
        w1_s = [tile([P, K_PASSES, PASS], U8, "w1_s%d" % b) for b in range(HALVES)]
        w3_s = [tile([P, K_PASSES, PASS], U8, "w3_s%d" % b) for b in range(HALVES)]
        w2_raw = {}
        for b in range(HALVES):
            for a in range(K_PASSES):
                width = PASS // 2 if (b, a) == (0, K_PASSES - 1) else PASS
                w2_raw[b, a] = [
                    (slice(c, c + width), tile([P, PACK, width], F32, "w2_raw%d%d_%d" % (b, a, c)))
                    for c in range(0, PASS, width)
                ]
        w2_bf = [tile([P, PASS, PACK], BF16, "w2_bf%d" % a) for a in range(K_PASSES)]
        w2_w = {(b, a): tile([P, PASS], U32, "w2_w%d%d" % (b, a)) for b in range(HALVES) for a in range(K_PASSES)}
        w2_s = {(b, a): tile([P, PASS], U8, "w2_s%d%d" % (b, a)) for b in range(HALVES) for a in range(K_PASSES)}

        y1 = [tile([P, 2, P, 2], F32, "y1_%d" % j) for j in range(J_TILES)]
        low = [tile([P, 2, P, 2], F32, "low%d" % j)[:] for j in range(J_TILES)]
        high = {(0, j): tile([P, S], F32, "high%d" % j) for j in range(J_TILES)}
        h = {(0, t): tile([P, S], F32, "h%d" % t) for t in range(PACK)}
        for i in range(PACK):
            high[1, i], h[1, i] = high[0, i], h[0, i]
        high[1, 0], h[1, 2] = h[0, 2], high[0, 0]

        page = {(b, t): tile([P, T2], F32, "page%d%d" % (b, t)) for b in range(HALVES) for t in range(PACK)}
        wg = [tile([P, S], F32, "wg0"), tile([P, S], F32, "wg1"), tile([P, 2, S], F32, "wg23")]
        picked = {(b, t): tile([P, NP], F32, "picked%d%d" % (b, t)) for b in range(HALVES) for t in range(PACK)}
        shifted = tile([P, NP], F32, "shifted")
        x1_planes = {(0, 0): tile([P, PACK, NP], F32, "x1_planes0")}
        x1_bf = {(0, 0): tile([P, NP, PACK], BF16, "x1_bf0")}
        x2_bf = [tile([P, NP, PACK], BF16, "x2_bf%d" % b) for b in range(HALVES)]
        x1_w = {}
        x1_w_second_half = tile([P, NP], U32, "x1_w1")
        for m in range(M_TILES):
            x1_w[1, m] = x1_w_second_half[:, P * m :]
        x2_w = [tile([P, NP], U32, "x2_w%d" % b) for b in range(HALVES)]
        x1_s = [tile([P, NP], U8, "x1_s%d" % b) for b in range(HALVES)]
        x2_s = [tile([P, NP], U8, "x2_s%d" % b) for b in range(HALVES)]
        bd_t = tile([P, HALVES, PACK], F32, "bd_t")
        gd_t = tile([P, HALVES, PACK], F32, "gd_t")
        rv_t = tile([P, M_TILES], F32, "rv_t")
        ident = tile([P, P], F32, "ident")

        def wgs_rows_of_slot(t):
            return wg[t][:] if t < 2 else wg[2][:, t - 2, :]

        def load_list(name, src):
            nc.sync.dma_start(lists[name][:], src)

        def load_scales(dst, src):
            for q in range(QUADRANTS):
                nc.sync.dma_start(
                    out=dst[32 * q : 32 * q + 4, :, :].bitcast(I32),
                    in_=src[:, 4 * q : 4 * q + 4, :].rearrange("a r c -> r a c").bitcast(I32),
                )

        def load_table(a):
            nc.sync.dma_start(out=tab_w[a][:].bitcast(I32), in_=tab_words[a].rearrange("p t i -> p (t i)").bitcast(I32))

        def load_w1(b):
            nc.sync.dma_start(
                out=w1_w[b][:].bitcast(I32),
                in_=w1_words[:, :, 2 * PASS * b : 2 * PASS * (b + 1)].rearrange("a p c -> p a c").bitcast(I32),
            )
            load_scales(w1_s[b], w1_scales[:, :, PASS * b : PASS * (b + 1)])

        def load_w3(b):
            nc.sync.dma_start(
                out=w3_w[b][:].bitcast(I32),
                in_=w3_words[:, :, PASS * b : PASS * (b + 1), :].rearrange("a p c i -> p a (c i)").bitcast(I32),
            )
            load_scales(w3_s[b], w3_scales[:, :, PASS * b : PASS * (b + 1)])

        def load_w2(b, a):
            rows = w2[PASS * a : PASS * (a + 1), PASS * b : PASS * (b + 1)].rearrange("(p i) c -> p i c", i=PACK)
            for cols, raw in w2_raw[b, a]:
                nc.sync.dma_start(out=raw[:], in_=rows[:, :, cols])

        def load_page(b, t):
            rows = page0[PASS * b : PASS * (b + 1), :].rearrange("(p t) c -> p t c", t=PACK)
            nc.sync.dma_start(out=page[b, t][:], in_=rows[:, t, :])

        def load_wgs(dst, slots):
            rows = wgs.rearrange("(q t) c -> q t c", t=PACK)
            for q in range(QUADRANTS):
                nc.sync.dma_start(out=dst[32 * q : 32 * (q + 1)], in_=rows[:, slots, :])

        nc.vector.memset(tab_s[:].bitcast(I32), 0)
        for b in range(HALVES):
            nc.vector.memset(w1_s[b][:].bitcast(I32), 0)
            nc.vector.memset(w3_s[b][:].bitcast(I32), 0)

        load_table(0)
        load_list("offs", offs)
        load_scales(tab_s, tab_scales)
        load_table(1)
        load_w1(0)
        load_w2(0, 0)
        load_w3(0)
        load_w2(0, 1)
        load_page(0, 0)
        load_wgs(wg[0], 0)
        load_wgs(wg[1], 1)
        load_page(0, 1)
        load_list("offs2", offs2)
        load_list("offs4", offs4)
        load_list("offs3", offs3)
        load_w1(1)
        load_w3(1)
        load_wgs(wg[2], slice(2, PACK))
        load_w2(1, 0)
        load_w2(1, 1)
        nc.sync.dma_start(out=bd_t[:], in_=bd.rearrange("(b p t) -> p b t", b=HALVES, t=PACK))
        nc.sync.dma_start(out=gd_t[:], in_=gd.rearrange("(b p t) -> p b t", b=HALVES, t=PACK))
        for t in range(2):
            load_page(1, t)
            load_page(0, 2 + t)
        for t in range(2, PACK):
            load_page(1, t)
        make_identity(nc, ident[:])

        for a in range(K_PASSES):
            nc.vector.tensor_copy(v_w[a][:], tab_w[a][:].indirect(lists["offs"][:]))
            nc.vector.tensor_copy(v_s[a][:], tab_s[:, a, :].indirect(lists["offs"][:]))

        def first_stage(acc, j, words, scales):
            cols = slice(P * j, P * (j + 1))
            for a in range(K_PASSES):
                nc.tensor.matmul_mx(
                    out=acc[:], lhsT=v_w[a][:, cols].bitcast(FP8X4), lhsT_scale=v_s[a][:, cols],
                    rhs=words(a), rhs_scale=scales(a), start=(a == 0), stop=(a == K_PASSES - 1),
                )

        def minima(b):
            for j in range(J_TILES):
                first_stage(bank[j], j, lambda a: w1_w[b][:, a, :].bitcast(FP4X4), lambda a: w1_s[b][:, a, :])
                first_stage(bank[UPPER + j], j, lambda a: w3_w[b][:, a, :].bitcast(FP8X4), lambda a: w3_s[b][:, a, :])
                nc.scalar.copy(out=y1[j][:], in_=by_word_pairs(bank[j]))
                nc.vector.tensor_tensor(low[j], by_word_pairs(bank[UPPER + j]), y1[j][:], ALU.min)

        def quantise_w2(b, a, copy):
            for cols, raw in w2_raw[b, a]:
                interleave(copy, w2_bf[a][:, cols, :], raw[:])
            nc.vector.quantize_mx(
                out=w2_w[b, a][:].bitcast(FP8X4), scales=w2_s[b, a][:],
                in_=w2_bf[a][:].rearrange("p c i -> p (c i)"),
            )

        def maxima(b):
            for j in range(J_TILES):
                first_stage(bank[UPPER + j], j, lambda a: w2_w[b, a][:].bitcast(FP8X4), lambda a: w2_s[b, a][:])
                nc.vector.tensor_tensor(as_pair_planes(high[b, j]), by_word_pairs(bank[UPPER + j]), y1[j][:], ALU.max)

        def features(b, t, acc, j0=0, j1=J_TILES, minima_first=False):
            if minima_first:
                terms = [(low[j], j) for j in range(j0, j1)] + [(as_pair_planes(high[b, j]), j) for j in range(j0, j1)]
            else:
                terms = [(term, j) for j in range(j0, j1) for term in (as_pair_planes(high[b, j]), low[j])]
            for n, (term, j) in enumerate(terms):
                nc.tensor.matmul(
                    out=acc[:, P * j : P * (j + 1)], lhsT=term[:, t // 2, :, t % 2], rhs=ident[:],
                    is_transpose=True, start=(n == 0), stop=(n == len(terms) - 1),
                )
            nc.scalar.copy(out=h[b, t][:, P * j0 : P * j1], in_=acc[:, P * j0 : P * j1])

        def put(b, t, j0=0, j1=J_TILES):
            cols = slice(P * j0, P * j1)
            entries = lists["offs2"][:, P * j0 // LIST_ROWS : P * j1 // LIST_ROWS]
            nc.vector.tensor_tensor(page[b, t][:].indirect(entries), h[b, t][:, cols], wgs_rows_of_slot(t)[:, cols], ALU.mult)

        def pick_classes(b, t, c0=0, c1=NP):
            entries = lists["offs4"][:, c0 // LIST_ROWS : c1 // LIST_ROWS]
            nc.vector.tensor_copy(picked[b, t][:, c0:c1], page[b, t][:].indirect(entries))

        def finish_classes(b, t, parts=1):
            width = NP // parts
            for c in range(0, NP, width):
                nc.scalar.activation(
                    out=shifted[:, c : c + width], in_=picked[b, t][:, c : c + width], func=ACT.Identity,
                    bias=bd_t[:, b, t : t + 1], scale=1.0,
                )
            for c in range(0, NP, width):
                nc.scalar.activation(
                    out=x2_bf[b][:, c : c + width, t], in_=shifted[:, c : c + width], func=ACT.Copy,
                    scale=gd_t[:, b, t : t + 1],
                )

        def pick_runs(b, t, m0, m1):
            entries = lists["offs3"][:, m0 // LIST_ROWS : m1 // LIST_ROWS]
            nc.vector.tensor_copy(x1_planes[b, m0][:, t, :], page[b, t][:].indirect(entries))

        def round_runs(b, m0):
            interleave(nc.scalar.copy, x1_bf[b, m0][:], x1_planes[b, m0][:])

        def quantise_runs(b, m0, m1, rounded):
            nc.vector.quantize_mx(
                out=x1_w[b, m0 // P][:, : m1 - m0].bitcast(FP8X4), scales=x1_s[b][:, m0:m1],
                in_=rounded.rearrange("p c i -> p (c i)"),
            )

        def quantise_classes(b):
            nc.vector.quantize_mx(
                out=x2_w[b][:].bitcast(FP8X4), scales=x2_s[b][:], in_=x2_bf[b][:].rearrange("p c i -> p (c i)"),
            )

        def match(b, m):
            cols = slice(P * m, P * (m + 1))
            nc.tensor.matmul_mx(
                out=bank[UPPER + m][:], lhsT=x1_w[b, m][:, :P].bitcast(FP8X4), lhsT_scale=x1_s[b][:, cols],
                rhs=x2_w[b][:].bitcast(FP8X4), rhs_scale=x2_s[b][:], start=(b == 0), stop=(b == HALVES - 1),
            )

        quantise_w2(0, 0, nc.vector.tensor_copy)
        minima(0)
        quantise_w2(0, 1, nc.scalar.copy)
        maxima(0)
        entry_parts = ((0, J_TILES // 2), (J_TILES // 2, J_TILES))
        for i, (j0, j1) in enumerate(entry_parts):
            for t in range(2):
                features(0, t, bank[2 * i + t], j0, j1, minima_first=(i == 0))
        features(0, 2, bank[UPPER + 3])
        features(0, 3, bank[UPPER + 2])
        for j0, j1 in entry_parts:
            for t in range(2):
                put(0, t, j0, j1)
        for t in range(2):
            pick_classes(0, t)
            pick_runs(0, t, 0, NP)

        minima(1)
        for a in range(K_PASSES):
            quantise_w2(1, a, nc.scalar.copy)
        put(0, 2)
        pick_classes(0, 2)
        for t in range(PACK - 1):
            finish_classes(0, t)
        maxima(1)
        put(0, 3)
        pick_runs(0, 2, 0, NP)
        pick_classes(0, 3)
        pick_runs(0, 3, 0, NP)
        for t in range(PACK - 1):
            features(1, t, bank[t], minima_first=(t == 0))
        finish_classes(0, 3)

        x1_planes[1, 0] = tile([P, PACK, 2 * P], F32, "x1_planes10", after="wg23")
        x1_planes[1, 2 * P] = tile([P, PACK, P], F32, "x1_planes12", after="h3")
        mat_t = tile([P, M_TILES, NP], F32, "mat_t", after="w2_raw00_0")
        result = tile([P, M_TILES, NP], F32, "result", after="w2_raw10_0")
        with nc.allow_non_contiguous_dma(reason="one value a partition"):
            nc.sync.dma_start(out=rv_t[:], in_=rv.rearrange("(m p) -> p m", p=P))
        nc.sync.dma_start(out=mat_t[:], in_=mat.rearrange("(m p) j -> p m j", p=P))

        put(1, 0)
        pick_classes(1, 0)
        round_runs(0, 0)
        features(1, 3, bank[3])
        finish_classes(1, 0)
        quantise_classes(0)
        for t in range(1, PACK - 1):
            put(1, t)
            pick_classes(1, t)
            finish_classes(1, t)
        put(1, 3)
        pick_classes(1, 3, 0, NP // 2)
        pick_classes(1, 3, NP // 2, NP)
        finish_classes(1, 3, parts=2)

        for i in range(2):
            words = tile([P, 2 * P], U32, "x1_w0%d" % i, after="picked1%d" % i)
            x1_w[0, 2 * i], x1_w[0, 2 * i + 1] = words[:], words[:, P:]
            quantise_runs(0, 2 * P * i, 2 * P * (i + 1), x1_bf[0, 0][:, 2 * P * i : 2 * P * (i + 1), :])
            match(0, 2 * i)
            match(0, 2 * i + 1)
        early_runs = tile([P, 3 * P, PACK], BF16, "x1_bf1_early", after="shifted")
        x1_bf[1, 0], x1_bf[1, 2 * P] = early_runs[:, : 2 * P, :], early_runs[:, 2 * P :, :]
        x1_bf[1, 3 * P] = tile([P, P, PACK], BF16, "x1_bf1_last")

        def pick_chunk(m0, m1):
            for t in range(PACK):
                pick_runs(1, t, P * m0, P * m1)

        def match_chunk(m0, m1):
            round_runs(1, P * m0)
            quantise_runs(1, P * m0, P * m1, x1_bf[1, P * m0][:])
            for m in range(m0, m1):
                match(1, m)

        def finish(m, cols):
            nc.vector.scalar_tensor_tensor(
                out=result[:, m, cols], in0=bank[UPPER + m][:, cols], scalar=rv_t[:, m : m + 1], in1=mat_t[:, m, cols],
                op0=ALU.add, op1=ALU.mult,
            )
            nc.sync.dma_start(out=out[P * m : P * (m + 1), cols], in_=result[:, m, cols])

        pick_chunk(0, 2)
        quantise_classes(1)
        pick_chunk(2, 3)
        match_chunk(0, 2)
        x1_planes[1, 3 * P] = tile([P, PACK, P], F32, "x1_planes13", after="wg23")
        pick_chunk(3, 4)
        match_chunk(2, 3)
        match_chunk(3, 4)
        for m in range(M_TILES - 1):
            finish(m, slice(0, NP))
        finish(M_TILES - 1, slice(0, NP // 2))
        finish(M_TILES - 1, slice(NP // 2, NP))
